import numpy as np
import ml_dtypes


def mxq(x, axis, fmt="e4m3"):
    dtype, down = {"e4m3": (ml_dtypes.float8_e4m3fn, 7), "e5m2": (ml_dtypes.float8_e5m2, 14)}[fmt]
    v = np.moveaxis(np.asarray(x, np.float32).astype(ml_dtypes.bfloat16).astype(np.float64), axis, -1)
    blocks = v.reshape(v.shape[:-1] + (-1, 32))
    amax = np.abs(blocks).max(-1, keepdims=True)
    byte = np.maximum(np.where(amax > 0, np.frexp(amax)[1] - 1 + 127, 0) - down, 1)
    scale = np.exp2(byte - 127.0)
    codes = (blocks / scale).astype(np.float32).astype(dtype).astype(np.float64)
    return np.moveaxis((codes * scale).reshape(v.shape), -1, axis)


WIDE = False


def mx_kscale(k):
    if not WIDE:
        return np.ones(k)
    levels = np.array([10, -10, 5, -5, 0])
    if k % 512:
        return np.exp2(np.random.permutation(np.resize(levels, k // 32))).repeat(32)
    a = np.empty((k // 512, 16))
    for p in range(k // 512):
        a[p, :8] = np.random.permutation(np.resize(levels, 8))
        for g in range(8):
            far = levels[np.abs(levels - a[p, g]) >= 10]
            a[p, g + 8] = far[np.random.randint(len(far))]
    return np.exp2(a.ravel()).repeat(32)


def f64(x):
    return np.asarray(x).astype(np.float64)


def striped(idx):
    return np.tile(idx.reshape(-1, 16).T, (8, 1)).astype(np.uint16)


def unstriped(offs):
    return offs[:16].T.reshape(-1).astype(np.int64)


K, T, D, S, V, N = 512, 1024, 3, 512, 256, 256


def setup_inputs():
    n = np.random.standard_normal
    s = mx_kscale(K)[:, None]
    return {
        "xT": (n((K, T)) * s).astype(np.float32),
        "w": (n((K, N)) / np.sqrt(K) / s).astype(np.float32),
        "b": (0.3 * n((N, 1))).astype(np.float32),
        "gate": np.tile(np.random.uniform(0.2, 1.0, (D, 1, V)) / np.sqrt(D), (1, N, 1)).astype(np.float32),
        "offs": striped(np.random.permutation(T)[:S]),
        "pos1": striped(np.random.permutation(S)[:V]),
        "pos2": striped(np.random.permutation(S)[:V]),
        "pos3": striped(np.random.permutation(S)[:V]),
    }


def reference(xT, w, b, gate, offs, pos1, pos2, pos3):
    idx = unstriped(offs)
    xq = mxq(f64(xT)[:, idx], 0, "e4m3")
    y = mxq(f64(w), 0, "e4m3").T @ xq
    y = y + f64(b)
    return sum(f64(gate[d]) * y[:, unstriped(p)] for d, p in enumerate((pos1, pos2, pos3)))

@@ -1,0 +1,141 @@
+from contextlib import ExitStack
+
+import concourse.mybir as mybir
+
+K, T, D, S, V, N = 512, 1024, 3, 512, 256, 256
+FLOPS = 2 * K * N * S
+
+F32 = mybir.dt.float32
+BF16 = mybir.dt.bfloat16
+U32 = mybir.dt.uint32
+U16 = mybir.dt.uint16
+U8 = mybir.dt.uint8
+FP8X4 = mybir.dt.float8_e4m3fn_x4
+IDENTITY = mybir.ActivationFunctionType.Identity
+MULT = mybir.AluOpType.mult
+ADD = mybir.AluOpType.add
+
+P = 128
+CHUNK = 512
+VECTOR_SHARE = 352
+HALF = S // 2
+
+
+def tile_picked_sub_lin_bias_sub_e_kernel(tc, xT, w, b, gate, offs, pos1, pos2, pos3, out):
+    nc = tc.nc
+    with ExitStack() as ctx:
+        keep = ctx.enter_context(tc.tile_pool(name="keep", bufs=1))
+        psum = ctx.enter_context(tc.psum_pool(name="psum", bufs=1))
+
+        warm_in = keep.tile([P, 8], F32, name="warm_in")
+        warm_out = keep.tile([P, 8], F32, name="warm_out")
+        nc.vector.memset(warm_in[:], 0.0)
+        nc.scalar.activation(warm_out[:], warm_in[:], IDENTITY, bias=warm_in[:, 0:1])
+
+        x_rows = xT.rearrange("(p u e) t -> p u e t", u=2, e=2)
+        raw = [[keep.tile([P, 2, CHUNK], F32, name="raw%d%d" % (u, c)) for c in range(2)] for u in range(2)]
+        offsets = keep.tile([P, S // 16], U16, name="offsets")
+        places = [keep.tile([P, V // 16], U16, name="places%d" % d) for d in range(D)]
+        w_raw = keep.tile([P, 4, N], F32, name="w_raw")
+        bias = keep.tile([P, 2], F32, name="bias")
+        gates = [keep.tile([P, D, V], F32, name="gates%d" % m) for m in range(2)]
+
+        nc.sync.dma_start(raw[0][0][:], x_rows[:, 0, :, 0:CHUNK])
+        nc.sync.dma_start(raw[0][1][:], x_rows[:, 0, :, CHUNK:T])
+        nc.sync.dma_start(offsets[:], offs)
+        nc.sync.dma_start(raw[1][0][:], x_rows[:, 1, :, 0:CHUNK])
+        nc.sync.dma_start(raw[1][1][:], x_rows[:, 1, :, CHUNK:T])
+        nc.sync.dma_start(w_raw[:], w.rearrange("(p j) c -> p j c", j=4))
+        with nc.allow_non_contiguous_dma(reason="one bias value a partition"):
+            nc.sync.dma_start(bias[:], b.rearrange("(m p) o -> p (m o)", p=P))
+        nc.sync.dma_start(gates[0][:], gate[:, 0:P, :].rearrange("d p v -> p d v"))
+        for d, pos in enumerate((pos1, pos2, pos3)):
+            nc.sync.dma_start(places[d][:], pos)
+        nc.sync.dma_start(gates[1][:], gate[:, P:N, :].rearrange("d p v -> p d v"))
+
+        pairs = [keep.tile([P, T, 2], BF16, name="pairs%d" % u, align_bytes=64) for u in range(2)]
+        picked = keep.tile([P, S, 4], BF16, name="picked", align_bytes=64)
+        picked_words = picked[:].rearrange("p s j -> p (s j)").bitcast(U32).rearrange("p (s u) -> p s u", u=2)
+
+        def pair_up(u, c, share):
+            src = raw[u][c][:].rearrange("p e t -> p t e")
+            t0 = c * CHUNK
+            if share:
+                nc.vector.tensor_copy(pairs[u][:, t0 : t0 + share, :], src[:, 0:share, :])
+            nc.scalar.copy(pairs[u][:, t0 + share : t0 + CHUNK, :], src[:, share:CHUNK, :])
+
+        def gather_pairs(u, s0, s1):
+            window = pairs[u][:].rearrange("p t e -> p (t e)").bitcast(U32)
+            nc.vector.tensor_copy(picked_words[:, s0:s1, u], window.indirect(offsets[:, s0 // 16 : s1 // 16]))
+
+        pair_up(0, 0, VECTOR_SHARE)
+        pair_up(0, 1, VECTOR_SHARE)
+        gather_pairs(0, 0, S)
+        pair_up(1, 0, 0)
+        pair_up(1, 1, VECTOR_SHARE)
+        gather_pairs(1, 0, HALF)
+        gather_pairs(1, HALF, S)
+
+        w_grouped = [keep.tile([P, P, 4], BF16, name="w_grouped%d" % m, align_bytes=64) for m in range(2)]
+        w_codes = [keep.tile([P, P], U32, name="w_codes%d" % m, align_bytes=64) for m in range(2)]
+        w_scales = [keep.tile([P, P], U8, name="w_scales%d" % m, align_bytes=64) for m in range(2)]
+        x_codes = [keep.tile([P, HALF], U32, name="x_codes%d" % h, align_bytes=64) for h in range(2)]
+        x_scales = [keep.tile([P, HALF], U8, name="x_scales%d" % h, align_bytes=64) for h in range(2)]
+        y = [keep.tile([P, S], F32, name="y%d" % m) for m in range(2)]
+
+        for m in range(2):
+            nc.scalar.copy(
+                w_grouped[m][:].rearrange("p (c i) j -> p c j i", i=4),
+                w_raw[:, :, m * P : (m + 1) * P].rearrange("p j (c i) -> p c j i", i=4),
+            )
+
+        def quantize_w(m):
+            nc.vector.quantize_mx(out=w_codes[m][:].bitcast(FP8X4), scales=w_scales[m][:],
+                                  in_=w_grouped[m][:].rearrange("p c j -> p (c j)"))
+
+        def quantize_x(h):
+            nc.vector.quantize_mx(out=x_codes[h][:].bitcast(FP8X4), scales=x_scales[h][:],
+                                  in_=picked[:, h * HALF : (h + 1) * HALF, :].rearrange("p s j -> p (s j)"))
+
+        def layer(m, h):
+            acc = psum.tile([P, HALF], F32, name="acc%d%d" % (m, h))
+            nc.tensor.matmul_mx(out=acc[:], lhsT=w_codes[m][:].bitcast(FP8X4), lhsT_scale=w_scales[m][:],
+                                rhs=x_codes[h][:].bitcast(FP8X4), rhs_scale=x_scales[h][:], start=True, stop=True)
+            nc.scalar.activation(y[m][:, h * HALF : (h + 1) * HALF], acc[:], IDENTITY, bias=bias[:, m : m + 1])
+
+        quantize_x(0)
+        quantize_w(0)
+        layer(0, 0)
+        quantize_x(1)
+        layer(0, 1)
+        quantize_w(1)
+        layer(1, 0)
+        layer(1, 1)
+
+        terms = [[keep.tile([P, V], F32, name="term%d%d" % (m, d)) for d in range(D)] for m in range(2)]
+        partial = [keep.tile([P, V], F32, name="partial%d" % m) for m in range(2)]
+        result = [keep.tile([P, V], F32, name="result%d" % m) for m in range(2)]
+
+        def neighbour(m, d, v0, v1):
+            nc.vector.tensor_tensor(terms[m][d][:, v0:v1], y[m][:].indirect(places[d][:, v0 // 16 : v1 // 16]),
+                                    gates[m][:, d, v0:v1], MULT)
+
+        def first_sum(m):
+            nc.vector.tensor_tensor(partial[m][:], terms[m][0][:], terms[m][1][:], ADD)
+
+        def last_sum(m, v0, v1):
+            nc.vector.tensor_tensor(result[m][:, v0:v1], partial[m][:, v0:v1], terms[m][2][:, v0:v1], ADD)
+            nc.sync.dma_start(out[m * P : (m + 1) * P, v0:v1], result[m][:, v0:v1])
+
+        neighbour(0, 0, 0, V)
+        neighbour(0, 1, 0, V)
+        neighbour(0, 2, 0, V)
+        first_sum(0)
+        neighbour(1, 0, 0, V)
+        neighbour(1, 1, 0, V)
+        last_sum(0, 0, V)
+        first_sum(1)
+        neighbour(1, 2, 0, V // 2)
+        neighbour(1, 2, V // 2, V)
+        last_sum(1, 0, V // 2)
+        last_sum(1, V // 2, V)

@@ -1,6 +1,7 @@
 from contextlib import ExitStack
 
 import concourse.mybir as mybir
+from concourse.masks import make_identity
 
 K, T, D, S, V, N = 512, 1024, 3, 512, 256, 256
 FLOPS = 2 * K * N * S
@@ -19,6 +20,7 @@ P = 128
 CHUNK = 512
 VECTOR_SHARE = 352
 HALF = S // 2
+PIECES = ((0, 256), (256, 384), (384, 512))
 
 
 def tile_picked_sub_lin_bias_sub_e_kernel(tc, xT, w, b, gate, offs, pos1, pos2, pos3, out):
@@ -31,6 +33,9 @@ def tile_picked_sub_lin_bias_sub_e_kernel(tc, xT, w, b, gate, offs, pos1, pos2, 
         warm_out = keep.tile([P, 8], F32, name="warm_out")
         nc.vector.memset(warm_in[:], 0.0)
         nc.scalar.activation(warm_out[:], warm_in[:], IDENTITY, bias=warm_in[:, 0:1])
+
+        identity = keep.tile([P, P], F32, name="identity")
+        make_identity(nc, identity[:])
 
         x_rows = xT.rearrange("(p u e) t -> p u e t", u=2, e=2)
         raw = [[keep.tile([P, 2, CHUNK], F32, name="raw%d%d" % (u, c)) for c in range(2)] for u in range(2)]
@@ -48,9 +53,9 @@ def tile_picked_sub_lin_bias_sub_e_kernel(tc, xT, w, b, gate, offs, pos1, pos2, 
         nc.sync.dma_start(w_raw[:], w.rearrange("(p j) c -> p j c", j=4))
         with nc.allow_non_contiguous_dma(reason="one bias value a partition"):
             nc.sync.dma_start(bias[:], b.rearrange("(m p) o -> p (m o)", p=P))
-        nc.sync.dma_start(gates[0][:], gate[:, 0:P, :].rearrange("d p v -> p d v"))
         for d, pos in enumerate((pos1, pos2, pos3)):
             nc.sync.dma_start(places[d][:], pos)
+        nc.sync.dma_start(gates[0][:], gate[:, 0:P, :].rearrange("d p v -> p d v"))
         nc.sync.dma_start(gates[1][:], gate[:, P:N, :].rearrange("d p v -> p d v"))
 
         pairs = [keep.tile([P, T, 2], BF16, name="pairs%d" % u, align_bytes=64) for u in range(2)]
@@ -79,8 +84,8 @@ def tile_picked_sub_lin_bias_sub_e_kernel(tc, xT, w, b, gate, offs, pos1, pos2, 
         w_grouped = [keep.tile([P, P, 4], BF16, name="w_grouped%d" % m, align_bytes=64) for m in range(2)]
         w_codes = [keep.tile([P, P], U32, name="w_codes%d" % m, align_bytes=64) for m in range(2)]
         w_scales = [keep.tile([P, P], U8, name="w_scales%d" % m, align_bytes=64) for m in range(2)]
-        x_codes = [keep.tile([P, HALF], U32, name="x_codes%d" % h, align_bytes=64) for h in range(2)]
-        x_scales = [keep.tile([P, HALF], U8, name="x_scales%d" % h, align_bytes=64) for h in range(2)]
+        x_codes = [keep.tile([P, s1 - s0], U32, name="x_codes%d" % s0, align_bytes=64) for s0, s1 in PIECES]
+        x_scales = [keep.tile([P, s1 - s0], U8, name="x_scales%d" % s0, align_bytes=64) for s0, s1 in PIECES]
         y = [keep.tile([P, S], F32, name="y%d" % m) for m in range(2)]
 
         for m in range(2):
@@ -94,48 +99,59 @@ def tile_picked_sub_lin_bias_sub_e_kernel(tc, xT, w, b, gate, offs, pos1, pos2, 
                                   in_=w_grouped[m][:].rearrange("p c j -> p (c j)"))
 
         def quantize_x(h):
+            s0, s1 = PIECES[h]
             nc.vector.quantize_mx(out=x_codes[h][:].bitcast(FP8X4), scales=x_scales[h][:],
-                                  in_=picked[:, h * HALF : (h + 1) * HALF, :].rearrange("p s j -> p (s j)"))
+                                  in_=picked[:, s0:s1, :].rearrange("p s j -> p (s j)"))
 
         def layer(m, h):
-            acc = psum.tile([P, HALF], F32, name="acc%d%d" % (m, h))
+            s0, s1 = PIECES[h]
+            acc = psum.tile([P, s1 - s0], F32, name="acc%d%d" % (m, h), tag="acc", bufs=4)
             nc.tensor.matmul_mx(out=acc[:], lhsT=w_codes[m][:].bitcast(FP8X4), lhsT_scale=w_scales[m][:],
                                 rhs=x_codes[h][:].bitcast(FP8X4), rhs_scale=x_scales[h][:], start=True, stop=True)
-            nc.scalar.activation(y[m][:, h * HALF : (h + 1) * HALF], acc[:], IDENTITY, bias=bias[:, m : m + 1])
+            nc.scalar.activation(y[m][:, s0:s1], acc[:], IDENTITY, bias=bias[:, m : m + 1])
 
         quantize_x(0)
         quantize_w(0)
         layer(0, 0)
         quantize_x(1)
         layer(0, 1)
+        quantize_x(2)
+        layer(0, 2)
         quantize_w(1)
         layer(1, 0)
         layer(1, 1)
+        layer(1, 2)
 
         terms = [[keep.tile([P, V], F32, name="term%d%d" % (m, d)) for d in range(D)] for m in range(2)]
-        partial = [keep.tile([P, V], F32, name="partial%d" % m) for m in range(2)]
+        partial = keep.tile([P, V], F32, name="partial")
         result = [keep.tile([P, V], F32, name="result%d" % m) for m in range(2)]
+        turned_sum = [psum.tile([P, P], F32, name="turned_sum%d" % q) for q in range(2)]
+        turned = keep.tile([P, 2, P], F32, name="turned")
+        upright = psum.tile([P, V], F32, name="upright")
 
         def neighbour(m, d, v0, v1):
             nc.vector.tensor_tensor(terms[m][d][:, v0:v1], y[m][:].indirect(places[d][:, v0 // 16 : v1 // 16]),
                                     gates[m][:, d, v0:v1], MULT)
 
-        def first_sum(m):
-            nc.vector.tensor_tensor(partial[m][:], terms[m][0][:], terms[m][1][:], ADD)
+        def last_sum(v0, v1):
+            nc.vector.tensor_tensor(result[1][:, v0:v1], partial[:, v0:v1], terms[1][2][:, v0:v1], ADD)
+            nc.sync.dma_start(out[P:N, v0:v1], result[1][:, v0:v1])
 
-        def last_sum(m, v0, v1):
-            nc.vector.tensor_tensor(result[m][:, v0:v1], partial[m][:, v0:v1], terms[m][2][:, v0:v1], ADD)
-            nc.sync.dma_start(out[m * P : (m + 1) * P, v0:v1], result[m][:, v0:v1])
+        for d in range(D):
+            neighbour(0, d, 0, V)
+            for q in range(2):
+                nc.tensor.matmul(turned_sum[q][:], lhsT=terms[0][d][:, q * P : (q + 1) * P], rhs=identity[:],
+                                 start=(d == 0), stop=(d == D - 1), is_transpose=True)
+        for q in range(2):
+            nc.scalar.copy(turned[:, q, :], turned_sum[q][:])
+            nc.tensor.transpose(upright[:, q * P : (q + 1) * P], turned[:, q, :], identity[:])
+        nc.scalar.copy(result[0][:], upright[:])
+        nc.sync.dma_start(out[0:P, :], result[0][:])
 
-        neighbour(0, 0, 0, V)
-        neighbour(0, 1, 0, V)
-        neighbour(0, 2, 0, V)
-        first_sum(0)
         neighbour(1, 0, 0, V)
         neighbour(1, 1, 0, V)
-        last_sum(0, 0, V)
-        first_sum(1)
         neighbour(1, 2, 0, V // 2)
+        nc.vector.tensor_tensor(partial[:], terms[1][0][:], terms[1][1][:], ADD)
         neighbour(1, 2, V // 2, V)
-        last_sum(1, 0, V // 2)
-        last_sum(1, V // 2, V)
+        last_sum(0, V // 2)
+        last_sum(V // 2, V)

@@ -20,6 +20,7 @@ P = 128
 CHUNK = 512
 VECTOR_SHARE = 352
 HALF = S // 2
+LAST_CUT = 192
 PIECES = ((0, 256), (256, 384), (384, 512))
 
 
@@ -38,18 +39,20 @@ def tile_picked_sub_lin_bias_sub_e_kernel(tc, xT, w, b, gate, offs, pos1, pos2, 
         make_identity(nc, identity[:])
 
         x_rows = xT.rearrange("(p u e) t -> p u e t", u=2, e=2)
-        raw = [[keep.tile([P, 2, CHUNK], F32, name="raw%d%d" % (u, c)) for c in range(2)] for u in range(2)]
+        raw_first = keep.tile([P, 2, T], F32, name="raw_first")
+        raw_second = [keep.tile([P, 2, CHUNK], F32, name="raw_second%d" % c) for c in range(2)]
         offsets = keep.tile([P, S // 16], U16, name="offsets")
         places = [keep.tile([P, V // 16], U16, name="places%d" % d) for d in range(D)]
         w_raw = keep.tile([P, 4, N], F32, name="w_raw")
         bias = keep.tile([P, 2], F32, name="bias")
         gates = [keep.tile([P, D, V], F32, name="gates%d" % m) for m in range(2)]
 
-        nc.sync.dma_start(raw[0][0][:], x_rows[:, 0, :, 0:CHUNK])
-        nc.sync.dma_start(raw[0][1][:], x_rows[:, 0, :, CHUNK:T])
+        nc.sync.dma_start(raw_first[:, 0, :], x_rows[:, 0, 0, :])
+        nc.sync.dma_start(raw_first[:, 1, 0:CHUNK], x_rows[:, 0, 1, 0:CHUNK])
+        nc.sync.dma_start(raw_first[:, 1, CHUNK:T], x_rows[:, 0, 1, CHUNK:T])
         nc.sync.dma_start(offsets[:], offs)
-        nc.sync.dma_start(raw[1][0][:], x_rows[:, 1, :, 0:CHUNK])
-        nc.sync.dma_start(raw[1][1][:], x_rows[:, 1, :, CHUNK:T])
+        nc.sync.dma_start(raw_second[0][:], x_rows[:, 1, :, 0:CHUNK])
+        nc.sync.dma_start(raw_second[1][:], x_rows[:, 1, :, CHUNK:T])
         nc.sync.dma_start(w_raw[:], w.rearrange("(p j) c -> p j c", j=4))
         with nc.allow_non_contiguous_dma(reason="one bias value a partition"):
             nc.sync.dma_start(bias[:], b.rearrange("(m p) o -> p (m o)", p=P))
@@ -62,30 +65,30 @@ def tile_picked_sub_lin_bias_sub_e_kernel(tc, xT, w, b, gate, offs, pos1, pos2, 
         picked = keep.tile([P, S, 4], BF16, name="picked", align_bytes=64)
         picked_words = picked[:].rearrange("p s j -> p (s j)").bitcast(U32).rearrange("p (s u) -> p s u", u=2)
 
-        def pair_up(u, c, share):
-            src = raw[u][c][:].rearrange("p e t -> p t e")
-            t0 = c * CHUNK
+        def pair_up(u, raw, t0, share):
+            src = raw.rearrange("p e t -> p t e")
+            width = src.shape[1]
             if share:
                 nc.vector.tensor_copy(pairs[u][:, t0 : t0 + share, :], src[:, 0:share, :])
-            nc.scalar.copy(pairs[u][:, t0 + share : t0 + CHUNK, :], src[:, share:CHUNK, :])
+            nc.scalar.copy(pairs[u][:, t0 + share : t0 + width, :], src[:, share:width, :])
 
         def gather_pairs(u, s0, s1):
             window = pairs[u][:].rearrange("p t e -> p (t e)").bitcast(U32)
             nc.vector.tensor_copy(picked_words[:, s0:s1, u], window.indirect(offsets[:, s0 // 16 : s1 // 16]))
 
-        pair_up(0, 0, VECTOR_SHARE)
-        pair_up(0, 1, VECTOR_SHARE)
+        pair_up(0, raw_first[:, :, 0:CHUNK], 0, VECTOR_SHARE)
+        pair_up(0, raw_first[:, :, CHUNK:T], CHUNK, VECTOR_SHARE)
         gather_pairs(0, 0, S)
-        pair_up(1, 0, 0)
-        pair_up(1, 1, VECTOR_SHARE)
+        pair_up(1, raw_second[0][:], 0, 0)
+        pair_up(1, raw_second[1][:], CHUNK, VECTOR_SHARE)
         gather_pairs(1, 0, HALF)
         gather_pairs(1, HALF, S)
 
         w_grouped = [keep.tile([P, P, 4], BF16, name="w_grouped%d" % m, align_bytes=64) for m in range(2)]
         w_codes = [keep.tile([P, P], U32, name="w_codes%d" % m, align_bytes=64) for m in range(2)]
         w_scales = [keep.tile([P, P], U8, name="w_scales%d" % m, align_bytes=64) for m in range(2)]
-        x_codes = [keep.tile([P, s1 - s0], U32, name="x_codes%d" % s0, align_bytes=64) for s0, s1 in PIECES]
-        x_scales = [keep.tile([P, s1 - s0], U8, name="x_scales%d" % s0, align_bytes=64) for s0, s1 in PIECES]
+        x_codes = keep.tile([P, S], U32, name="x_codes", align_bytes=64)
+        x_scales = keep.tile([P, S], U8, name="x_scales", align_bytes=64)
         y = [keep.tile([P, S], F32, name="y%d" % m) for m in range(2)]
 
         for m in range(2):
@@ -98,29 +101,24 @@ def tile_picked_sub_lin_bias_sub_e_kernel(tc, xT, w, b, gate, offs, pos1, pos2, 
             nc.vector.quantize_mx(out=w_codes[m][:].bitcast(FP8X4), scales=w_scales[m][:],
                                   in_=w_grouped[m][:].rearrange("p c j -> p (c j)"))
 
-        def quantize_x(h):
-            s0, s1 = PIECES[h]
-            nc.vector.quantize_mx(out=x_codes[h][:].bitcast(FP8X4), scales=x_scales[h][:],
+        def quantize_x(s0, s1):
+            nc.vector.quantize_mx(out=x_codes[:, s0:s1].bitcast(FP8X4), scales=x_scales[:, s0:s1],
                                   in_=picked[:, s0:s1, :].rearrange("p s j -> p (s j)"))
 
-        def layer(m, h):
-            s0, s1 = PIECES[h]
-            acc = psum.tile([P, s1 - s0], F32, name="acc%d%d" % (m, h), tag="acc", bufs=4)
+        def layer(m, s0, s1):
+            acc = psum.tile([P, s1 - s0], F32, name="acc%d_%d" % (m, s0))
             nc.tensor.matmul_mx(out=acc[:], lhsT=w_codes[m][:].bitcast(FP8X4), lhsT_scale=w_scales[m][:],
-                                rhs=x_codes[h][:].bitcast(FP8X4), rhs_scale=x_scales[h][:], start=True, stop=True)
+                                rhs=x_codes[:, s0:s1].bitcast(FP8X4), rhs_scale=x_scales[:, s0:s1], start=True, stop=True)
             nc.scalar.activation(y[m][:, s0:s1], acc[:], IDENTITY, bias=bias[:, m : m + 1])
 
-        quantize_x(0)
+        quantize_x(*PIECES[0])
         quantize_w(0)
-        layer(0, 0)
-        quantize_x(1)
-        layer(0, 1)
-        quantize_x(2)
-        layer(0, 2)
+        layer(0, *PIECES[0])
+        for piece in PIECES[1:]:
+            quantize_x(*piece)
+            layer(0, *piece)
         quantize_w(1)
-        layer(1, 0)
-        layer(1, 1)
-        layer(1, 2)
+        layer(1, 0, S)
 
         terms = [[keep.tile([P, V], F32, name="term%d%d" % (m, d)) for d in range(D)] for m in range(2)]
         partial = keep.tile([P, V], F32, name="partial")
@@ -146,12 +144,12 @@ def tile_picked_sub_lin_bias_sub_e_kernel(tc, xT, w, b, gate, offs, pos1, pos2, 
             nc.scalar.copy(turned[:, q, :], turned_sum[q][:])
             nc.tensor.transpose(upright[:, q * P : (q + 1) * P], turned[:, q, :], identity[:])
         nc.scalar.copy(result[0][:], upright[:])
-        nc.sync.dma_start(out[0:P, :], result[0][:])
+        nc.scalar.dma_start(out[0:P, :], result[0][:])
 
         neighbour(1, 0, 0, V)
         neighbour(1, 1, 0, V)
-        neighbour(1, 2, 0, V // 2)
+        neighbour(1, 2, 0, LAST_CUT)
         nc.vector.tensor_tensor(partial[:], terms[1][0][:], terms[1][1][:], ADD)
-        neighbour(1, 2, V // 2, V)
-        last_sum(0, V // 2)
-        last_sum(V // 2, V)
+        neighbour(1, 2, LAST_CUT, V)
+        last_sum(0, LAST_CUT)
+        last_sum(LAST_CUT, V)

@@ -18,7 +18,7 @@ ADD = mybir.AluOpType.add
 
 P = 128
 CHUNK = 512
-VECTOR_SHARE = 352
+VECTOR_SHARE = 400
 HALF = S // 2
 LAST_CUT = 192
 PIECES = ((0, 256), (256, 384), (384, 512))
@@ -84,10 +84,14 @@ def tile_picked_sub_lin_bias_sub_e_kernel(tc, xT, w, b, gate, offs, pos1, pos2, 
         gather_pairs(1, 0, HALF)
         gather_pairs(1, HALF, S)
 
-        w_grouped = [keep.tile([P, P, 4], BF16, name="w_grouped%d" % m, align_bytes=64) for m in range(2)]
+        w_grouped = [keep.tile([P, P, 4], BF16, name="w_grouped%d" % m, tag="shared%d" % m, align_bytes=64) for m in range(2)]
         w_codes = [keep.tile([P, P], U32, name="w_codes%d" % m, align_bytes=64) for m in range(2)]
         w_scales = [keep.tile([P, P], U8, name="w_scales%d" % m, align_bytes=64) for m in range(2)]
-        x_codes = keep.tile([P, S], U32, name="x_codes", align_bytes=64)
+        x_codes = [keep.tile([P, HALF], U32, name="x_codes0", align_bytes=64)]
+
+        def codes(s0, s1):
+            return x_codes[s0 // HALF][:, s0 % HALF : s0 % HALF + s1 - s0].bitcast(FP8X4)
+
         x_scales = keep.tile([P, S], U8, name="x_scales", align_bytes=64)
         y = [keep.tile([P, S], F32, name="y%d" % m) for m in range(2)]
 
@@ -102,23 +106,30 @@ def tile_picked_sub_lin_bias_sub_e_kernel(tc, xT, w, b, gate, offs, pos1, pos2, 
                                   in_=w_grouped[m][:].rearrange("p c j -> p (c j)"))
 
         def quantize_x(s0, s1):
-            nc.vector.quantize_mx(out=x_codes[:, s0:s1].bitcast(FP8X4), scales=x_scales[:, s0:s1],
+            nc.vector.quantize_mx(out=codes(s0, s1), scales=x_scales[:, s0:s1],
                                   in_=picked[:, s0:s1, :].rearrange("p s j -> p (s j)"))
+
+        def product(acc, m, s0, s1):
+            nc.tensor.matmul_mx(out=acc, lhsT=w_codes[m][:].bitcast(FP8X4), lhsT_scale=w_scales[m][:],
+                                rhs=codes(s0, s1), rhs_scale=x_scales[:, s0:s1], start=True, stop=True)
 
         def layer(m, s0, s1):
             acc = psum.tile([P, s1 - s0], F32, name="acc%d_%d" % (m, s0))
-            nc.tensor.matmul_mx(out=acc[:], lhsT=w_codes[m][:].bitcast(FP8X4), lhsT_scale=w_scales[m][:],
-                                rhs=x_codes[:, s0:s1].bitcast(FP8X4), rhs_scale=x_scales[:, s0:s1], start=True, stop=True)
+            product(acc[:], m, s0, s1)
             nc.scalar.activation(y[m][:, s0:s1], acc[:], IDENTITY, bias=bias[:, m : m + 1])
 
         quantize_x(*PIECES[0])
         quantize_w(0)
         layer(0, *PIECES[0])
+        x_codes.append(keep.tile([P, HALF], U32, name="x_codes1", tag="shared0", align_bytes=64))
         for piece in PIECES[1:]:
             quantize_x(*piece)
             layer(0, *piece)
         quantize_w(1)
-        layer(1, 0, S)
+        acc = psum.tile([P, S], F32, name="acc1")
+        for s0 in (0, HALF):
+            product(acc[:, s0 : s0 + HALF], 1, s0, s0 + HALF)
+        nc.scalar.activation(y[1][:], acc[:], IDENTITY, bias=bias[:, 1:2])
 
         terms = [[keep.tile([P, V], F32, name="term%d%d" % (m, d)) for d in range(D)] for m in range(2)]
         partial = keep.tile([P, V], F32, name="partial")

from contextlib import ExitStack

import concourse.mybir as mybir
from concourse.masks import make_identity

K, T, D, S, V, N = 512, 1024, 3, 512, 256, 256
FLOPS = 2 * K * N * S

F32 = mybir.dt.float32
BF16 = mybir.dt.bfloat16
U32 = mybir.dt.uint32
U16 = mybir.dt.uint16
U8 = mybir.dt.uint8
FP8X4 = mybir.dt.float8_e4m3fn_x4
IDENTITY = mybir.ActivationFunctionType.Identity
MULT = mybir.AluOpType.mult
ADD = mybir.AluOpType.add

P = 128
CHUNK = 512
VECTOR_SHARE = 400
HALF = S // 2
LAST_CUT = 192
PIECES = ((0, 256), (256, 384), (384, 512))


def tile_picked_sub_lin_bias_sub_e_kernel(tc, xT, w, b, gate, offs, pos1, pos2, pos3, out):
    nc = tc.nc
    with ExitStack() as ctx:
        keep = ctx.enter_context(tc.tile_pool(name="keep", bufs=1))
        psum = ctx.enter_context(tc.psum_pool(name="psum", bufs=1))

        warm_in = keep.tile([P, 8], F32, name="warm_in")
        warm_out = keep.tile([P, 8], F32, name="warm_out")
        nc.vector.memset(warm_in[:], 0.0)
        nc.scalar.activation(warm_out[:], warm_in[:], IDENTITY, bias=warm_in[:, 0:1])

        identity = keep.tile([P, P], F32, name="identity")
        make_identity(nc, identity[:])

        x_rows = xT.rearrange("(p u e) t -> p u e t", u=2, e=2)
        raw_first = keep.tile([P, 2, T], F32, name="raw_first")
        raw_second = [keep.tile([P, 2, CHUNK], F32, name="raw_second%d" % c) for c in range(2)]
        offsets = keep.tile([P, S // 16], U16, name="offsets")
        places = [keep.tile([P, V // 16], U16, name="places%d" % d) for d in range(D)]
        w_raw = keep.tile([P, 4, N], F32, name="w_raw")
        bias = keep.tile([P, 2], F32, name="bias")
        gates = [keep.tile([P, D, V], F32, name="gates%d" % m) for m in range(2)]

        nc.sync.dma_start(raw_first[:, 0, :], x_rows[:, 0, 0, :])
        nc.sync.dma_start(raw_first[:, 1, 0:CHUNK], x_rows[:, 0, 1, 0:CHUNK])
        nc.sync.dma_start(raw_first[:, 1, CHUNK:T], x_rows[:, 0, 1, CHUNK:T])
        nc.sync.dma_start(offsets[:], offs)
        nc.sync.dma_start(raw_second[0][:], x_rows[:, 1, :, 0:CHUNK])
        nc.sync.dma_start(raw_second[1][:], x_rows[:, 1, :, CHUNK:T])
        nc.sync.dma_start(w_raw[:], w.rearrange("(p j) c -> p j c", j=4))
        with nc.allow_non_contiguous_dma(reason="one bias value a partition"):
            nc.sync.dma_start(bias[:], b.rearrange("(m p) o -> p (m o)", p=P))
        for d, pos in enumerate((pos1, pos2, pos3)):
            nc.sync.dma_start(places[d][:], pos)
        nc.sync.dma_start(gates[0][:], gate[:, 0:P, :].rearrange("d p v -> p d v"))
        nc.sync.dma_start(gates[1][:], gate[:, P:N, :].rearrange("d p v -> p d v"))

        pairs = [keep.tile([P, T, 2], BF16, name="pairs%d" % u, align_bytes=64) for u in range(2)]
        picked = keep.tile([P, S, 4], BF16, name="picked", align_bytes=64)
        picked_words = picked[:].rearrange("p s j -> p (s j)").bitcast(U32).rearrange("p (s u) -> p s u", u=2)

        def pair_up(u, raw, t0, share):
            src = raw.rearrange("p e t -> p t e")
            width = src.shape[1]
            if share:
                nc.vector.tensor_copy(pairs[u][:, t0 : t0 + share, :], src[:, 0:share, :])
            nc.scalar.copy(pairs[u][:, t0 + share : t0 + width, :], src[:, share:width, :])

        def gather_pairs(u, s0, s1):
            window = pairs[u][:].rearrange("p t e -> p (t e)").bitcast(U32)
            nc.vector.tensor_copy(picked_words[:, s0:s1, u], window.indirect(offsets[:, s0 // 16 : s1 // 16]))

        pair_up(0, raw_first[:, :, 0:CHUNK], 0, VECTOR_SHARE)
        pair_up(0, raw_first[:, :, CHUNK:T], CHUNK, VECTOR_SHARE)
        gather_pairs(0, 0, S)
        pair_up(1, raw_second[0][:], 0, 0)
        pair_up(1, raw_second[1][:], CHUNK, VECTOR_SHARE)
        gather_pairs(1, 0, HALF)
        gather_pairs(1, HALF, S)

        w_grouped = [keep.tile([P, P, 4], BF16, name="w_grouped%d" % m, tag="shared%d" % m, align_bytes=64) for m in range(2)]
        w_codes = [keep.tile([P, P], U32, name="w_codes%d" % m, align_bytes=64) for m in range(2)]
        w_scales = [keep.tile([P, P], U8, name="w_scales%d" % m, align_bytes=64) for m in range(2)]
        x_codes = [keep.tile([P, HALF], U32, name="x_codes0", align_bytes=64)]

        def codes(s0, s1):
            return x_codes[s0 // HALF][:, s0 % HALF : s0 % HALF + s1 - s0].bitcast(FP8X4)

        x_scales = keep.tile([P, S], U8, name="x_scales", align_bytes=64)
        y = [keep.tile([P, S], F32, name="y%d" % m) for m in range(2)]

        for m in range(2):
            nc.scalar.copy(
                w_grouped[m][:].rearrange("p (c i) j -> p c j i", i=4),
                w_raw[:, :, m * P : (m + 1) * P].rearrange("p j (c i) -> p c j i", i=4),
            )

        def quantize_w(m):
            nc.vector.quantize_mx(out=w_codes[m][:].bitcast(FP8X4), scales=w_scales[m][:],
                                  in_=w_grouped[m][:].rearrange("p c j -> p (c j)"))

        def quantize_x(s0, s1):
            nc.vector.quantize_mx(out=codes(s0, s1), scales=x_scales[:, s0:s1],
                                  in_=picked[:, s0:s1, :].rearrange("p s j -> p (s j)"))

        def product(acc, m, s0, s1):
            nc.tensor.matmul_mx(out=acc, lhsT=w_codes[m][:].bitcast(FP8X4), lhsT_scale=w_scales[m][:],
                                rhs=codes(s0, s1), rhs_scale=x_scales[:, s0:s1], start=True, stop=True)

        def layer(m, s0, s1):
            acc = psum.tile([P, s1 - s0], F32, name="acc%d_%d" % (m, s0))
            product(acc[:], m, s0, s1)
            nc.scalar.activation(y[m][:, s0:s1], acc[:], IDENTITY, bias=bias[:, m : m + 1])

        quantize_x(*PIECES[0])
        quantize_w(0)
        layer(0, *PIECES[0])
        x_codes.append(keep.tile([P, HALF], U32, name="x_codes1", tag="shared0", align_bytes=64))
        for piece in PIECES[1:]:
            quantize_x(*piece)
            layer(0, *piece)
        quantize_w(1)
        acc = psum.tile([P, S], F32, name="acc1")
        for s0 in (0, HALF):
            product(acc[:, s0 : s0 + HALF], 1, s0, s0 + HALF)
        nc.scalar.activation(y[1][:], acc[:], IDENTITY, bias=bias[:, 1:2])

        terms = [[keep.tile([P, V], F32, name="term%d%d" % (m, d)) for d in range(D)] for m in range(2)]
        partial = keep.tile([P, V], F32, name="partial")
        result = [keep.tile([P, V], F32, name="result%d" % m) for m in range(2)]
        turned_sum = [psum.tile([P, P], F32, name="turned_sum%d" % q) for q in range(2)]
        turned = keep.tile([P, 2, P], F32, name="turned")
        upright = psum.tile([P, V], F32, name="upright")

        def neighbour(m, d, v0, v1):
            nc.vector.tensor_tensor(terms[m][d][:, v0:v1], y[m][:].indirect(places[d][:, v0 // 16 : v1 // 16]),
                                    gates[m][:, d, v0:v1], MULT)

        def last_sum(v0, v1):
            nc.vector.tensor_tensor(result[1][:, v0:v1], partial[:, v0:v1], terms[1][2][:, v0:v1], ADD)
            nc.sync.dma_start(out[P:N, v0:v1], result[1][:, v0:v1])

        for d in range(D):
            neighbour(0, d, 0, V)
            for q in range(2):
                nc.tensor.matmul(turned_sum[q][:], lhsT=terms[0][d][:, q * P : (q + 1) * P], rhs=identity[:],
                                 start=(d == 0), stop=(d == D - 1), is_transpose=True)
        for q in range(2):
            nc.scalar.copy(turned[:, q, :], turned_sum[q][:])
            nc.tensor.transpose(upright[:, q * P : (q + 1) * P], turned[:, q, :], identity[:])
        nc.scalar.copy(result[0][:], upright[:])
        nc.scalar.dma_start(out[0:P, :], result[0][:])

        neighbour(1, 0, 0, V)
        neighbour(1, 1, 0, V)
        neighbour(1, 2, 0, LAST_CUT)
        nc.vector.tensor_tensor(partial[:], terms[1][0][:], terms[1][1][:], ADD)
        neighbour(1, 2, LAST_CUT, V)
        last_sum(0, LAST_CUT)
        last_sum(LAST_CUT, V)
